import numpy as np, ml_dtypes
CORES = [16,18,20,22]
N = 4
BF = ml_dtypes.bfloat16
def gentries(a):
    return np.ascontiguousarray(a.reshape(8, 16, -1).transpose(0, 2, 1)).reshape(8, -1)
def gtable(e):
    e = np.asarray(e); return np.ascontiguousarray(e.reshape(8, -1, 16).transpose(0, 2, 1)).reshape(128, -1).astype(np.int32)
def f(rng, *shape):
    return (rng.standard_normal(shape, dtype=np.float32) * np.exp2(rng.integers(-2, 3, shape[:-1] + (1,)))).astype(BF)
def wide(rng, *shape):
    v = f(rng, *shape).astype(np.float32); k = shape[:-2] + (1, shape[-1])
    return (v * np.exp2(rng.integers(-6, 7, k)) * (rng.random(k) > 0.0625)).astype(BF)
W, C, D, B, R, K = 8192, 1024, 6, 4, 12, 101
def ints(x):
    return np.clip(np.rint(x), -32768, 32768).astype(BF)
def cols(fr, ix):
    return np.take_along_axis(fr.reshape(N, 8, 16, W), ix[None, :, None, :], 3).astype(np.float32).astype(np.int64)
def limits(rng, fr):
    m = 512; lim = np.zeros((8, 16, D), np.int64); s = cols(fr, rng.integers(0, W, (8, m)))
    for l in range(D):
        s = s + cols(fr, rng.integers(0, W, (8, m))); en = np.sum(np.abs(s), axis=(0, 2)); o = np.argsort(en, axis=1)
        lim[:, :, l] = np.take_along_axis(np.take_along_axis(en, o, 1), rng.integers(m // 5, 4 * m // 5, (8, 16)), 1)
        s = np.take_along_axis(s, o[:, rng.integers(0, m // 2, m)][None, :, None, :], 3)
    return lim
def parts(rng):
    fr = ints(f(rng, N, 128, W).astype(np.float32) * 1024)
    return fr, rng.integers(0, W, (8, W)), rng.integers(0, W, (8, C))
def pack(fr, first, start, lim):
    return {"frag": fr, "first": np.stack([first.astype(np.int32)] * N), "start": np.stack([gtable(start)] * N), "lim": np.stack([lim.reshape(128, D).astype(np.int32)] * N)}
def setup_inputs(rng):
    fr, first, start = parts(rng)
    return pack(fr, first, start, limits(rng, fr))
def setup_inputs_ties(rng):
    fr, first, start = parts(rng); x = fr.reshape(N, 8, 16, W)
    x[:, ::2] = (4096 * rng.integers(-1, 2, (N, 4, 16, W))).astype(np.float32).astype(BF)
    x[..., 0] = 0; x[..., W - 1] = 0; x[..., 5] = -x[..., 7]
    first[:, 0] = W - 1; first[:, W - 1] = 0; first[:, 5] = 7; start[::2, 15::32] = 0; start[::2, 14::32] = 5
    lim = limits(rng, fr); lim[::2] = np.maximum(lim[::2] - rng.integers(0, 2, (4, 16, D)), 0)
    lim[::2, 15] = 0; lim[::2, 14, 0] = 0
    s = cols(fr, start[:, :16]) + cols(fr, np.take_along_axis(first, start[:, :16], 1)); en = np.sum(np.abs(s), axis=(0, 2))
    lim[1::2, :, 0] = np.maximum(en - (np.arange(16) & 1), 0)[1::2]
    return pack(fr, first, start, lim)
def setup_inputs_walls(rng):
    fr, first, start = parts(rng); lim = limits(rng, fr)
    m = ((np.arange(16)[None, :] + rng.integers(0, 16, (8, 1))) % (D + 1))[:, :, None]; lv = np.arange(D)[None, None, :]
    lim = np.where((lv < m) & (rng.random((8, 16, 1)) < 0.6), 2 ** 24 - 1, lim)
    return pack(fr, first, start, np.where(lv == m, 0, lim))
def setup_inputs_alike(rng):
    fr, first, start = parts(rng); lim = limits(rng, fr)
    start[::2] = rng.choice(np.array([0, W - 1, W // 2, 3]), (4, C))
    first[1] = np.arange(W); first[2] = rng.choice(np.array([0, W - 1, W - K, W - K - 1, W - K + 1]), W)
    first[4] = np.where(rng.random(W) < 0.5, W - K, first[4]); first[5] = W - 1 - rng.integers(0, K, W); start[6, ::2] = W - 1
    return pack(fr, first, start, lim)
def setup_inputs_ends(rng):
    fr, first, start = parts(rng); x = fr.reshape(N, 8, 16, W); lv = np.arange(1, D + 1)[None, :]; odd = (np.arange(16) & 1)[:, None]
    x[:, 3] = (32768 * (2 * rng.integers(0, 2, (N, 16, 1)) - 1) * np.where(rng.random(W) < 0.9, 1, -1)).astype(np.float32).astype(BF)
    x[:, 4::3] = np.where(rng.random((N, 2, 16, W)) < 0.5, rng.integers(-255, 256, (N, 2, 16, W)), rng.choice(np.array([-32768, 32768]), (N, 2, 16, W))).astype(np.float32).astype(BF)
    x[:, 5] = rng.integers(-255, 256, (N, 16, W)).astype(np.float32).astype(BF)
    x[int(rng.integers(0, N)), 5] = (32768 * (2 * rng.integers(0, 2, (16, 1)) - 1)).astype(np.float32).astype(BF)
    lim = limits(rng, fr)
    lim[0] = 0; lim[1] = 2 ** 24 - 1; lim[2] = 2 ** 24 - 1; lim[2, :, D - 1] = 0; lim[7, :2] = 2 ** 24 - 1
    lim[3] = 2 ** 21 * (lv + 1) - odd * (lv >= 4)
    lim[5] = 2 ** 19 * (lv + 1) + 2 ** 17
    lim[5, ::2, 3] = rng.integers(2 ** 21 + 2 ** 17, 5 * 2 ** 19, 8)
    if D > 4: lim[5, 1::2, 4] = rng.integers(2 ** 21 + 2 ** 17, 6 * 2 ** 19, 8)
    s = cols(fr, start) + cols(fr, np.take_along_axis(first, start, 1)); sh = np.sum(np.abs(s[:, 4]), axis=1)
    hi = sh.astype(np.float32).astype(BF).astype(np.float64); lo = (sh - hi).astype(np.float32).astype(BF).astype(np.float64); er = np.sum(hi + lo - sh, axis=0)
    for i in range(16):
        c = i + 16 * int(np.argmin(er[i::16]) if i & 1 else np.argmax(er[i::16]))
        lim[4, i, 0] = np.sum(sh[:, c]) - (i & 1)
    return pack(fr, first, start, lim)
def setup_inputs_spread(rng):
    fr, first, start = parts(rng); fr = ints(wide(rng, N, 128, W).astype(np.float32) * 32)
    return pack(fr, first, start, limits(rng, fr))
def check_inputs(d):
    bad = []; v = np.asarray(d["frag"]).astype(np.float32)
    if not np.all((np.abs(v) <= 32768) & (np.rint(v) == v)): bad.append("frag: whole numbers from -32768 to 32768")
    for k, hi in (("first", W - 1), ("start", W - 1), ("lim", 2 ** 24 - 1)):
        if np.min(d[k]) < 0 or np.max(d[k]) > hi: bad.append("range of " + k)
        if np.any(d[k] != d[k][:1]): bad.append(k + " is not alike on all ranks")
    return bad
def reference(frag, first, start, lim):
    fr = frag.astype(np.float32).astype(np.int32).reshape(N, 8, 16, W).transpose(1, 3, 0, 2).reshape(8, W, 16 * N)
    fi = first[0].astype(np.int64); lm = lim[0].astype(np.int64).reshape(8, 16, D)
    M = 8 * C; a = np.arange(M); g = np.repeat(np.arange(8), C); cl = np.tile(np.arange(C) & 15, 8)
    V = np.zeros((M, D + 1), np.int64); Q = np.zeros((M, D + 1), np.int64); S = np.zeros((M, D + 1, 16 * N), np.int32); d = np.zeros(M, np.int64)
    V[:, 0] = gentries(start[0]).reshape(-1); S[:, 0] = fr[g, V[:, 0]]
    for rnd in range(R):
        v = V[a, d]; b = Q[a, d]; live = d < D
        w = (fi[g, v] + K * b) & (W - 1)
        s = S[a, d] + fr[g, w]; en = np.sum(np.abs(s), axis=1); up = np.minimum(d + 1, D)
        go = live & (b < B) & (en <= lm[g, cl, up - 1]); no = live & (b < B) & ~go
        back = live & (b == B) & (d > 0); anew = live & (b == B) & (d == 0)
        Q[a[no], d[no]] += 1
        Q[a[anew], 0] = 0
        Q[a[back], d[back] - 1] += 1
        V[a[go], up[go]] = w[go]; Q[a[go], up[go]] = 0; S[a[go], up[go]] = s[go]
        d = d + go.astype(np.int64) - back.astype(np.int64)
    y = S[a, d].reshape(8, C, N, 16).transpose(2, 0, 3, 1).reshape(N, 128, C)
    t = np.where(np.arange(D + 1)[None, :] <= d[:, None], 16 * V + Q, -1).reshape(8, C, D + 1).transpose(0, 2, 1).reshape(8, -1)
    return {"y": np.ascontiguousarray(y).astype(np.float32), "stk": np.stack([gtable(t)] * N).astype(np.float32)}

import numpy as np
from concourse.bass import DstId, RemoteDMATransfer
from concourse.mybir import AluOpType, ActivationFunctionType

NR, NCY, W, STEP = 4, 6, 8192, 101
BIG = float(2 ** 23)
SCRATCH = {}
for _n, _s, _t in [("fr", [W], "bfloat16"), ("ft", [W], "bfloat16"), ("fi", [512], "int32"), ("fh", [512], "bfloat16"), ("fl", [512], "bfloat16"),
                   ("S", [1024], "float32"), ("ab", [3072], "float32"), ("Y", [1024], "float32"), ("I", [1792], "int32"), ("F", [6144], "float32"),
                   ("U", [2048], "uint16"), ("B", [4096], "bfloat16"), ("sk", [7, 64], "float32"), ("xl", [4, 48], "float32"), ("xs", [4, 96], "float32")]:
    SCRATCH[_n] = ("sbuf", [128] + _s, _t)
for _n in ["pa", "pb", "pt", "pm", "pe0", "pe1", "pe2", "pe3"]:
    SCRATCH[_n] = ("psum", [128, 512], "float32")
for _q in range(NR):
    SCRATCH["L%d" % _q] = ("sbuf", [128, (3 * NCY + 1) * 256], "float32")
for _c in range(1, NCY + 1):
    SCRATCH["cs%d" % _c] = ("sbuf", [128, 4, 128], "int32")
    SCRATCH["cl%d" % _c] = ("sbuf", [128, 4, 48], "int32")

SEMAPHORES = ["cv", "ca", "cp", "cg", "sent"] + ["d%d" % i for i in range(16)] + ["pr%d" % c for c in range(1, NCY + 1)] \
    + ["la%d_%d" % (c, q) for c in range(1, NCY + 2) for q in range(NR)] + ["lb%d_%d" % (c, q) for c in range(1, NCY + 2) for q in range(NR)]

A = AluOpType
ACT = ActivationFunctionType
PAR = {"cy": 1.04, "one": 2400.0, "all": 3200.0, "issue": 600.0, "shift": 1500.0, "noise": 300.0, "seed": 1}
_PLAN = {}


def D(buf, *idx):
    return (buf, tuple(slice(x[0], x[0] + x[1]) if isinstance(x, tuple) else x for x in idx))


def sub(d, a, n, step=1):
    a += d[1][0].start
    return (d[0], (slice(a, a + (n - 1) * step + 1, step) if step > 1 else slice(a, a + n),))


def cols(d):
    shape = SCRATCH[d[0]][1][1:]
    return np.arange(int(np.prod(shape))).reshape(shape)[d[1]].reshape(-1)


def bits(d):
    c = cols(d)
    lo, hi = int(c.min()), int(c.max())
    if hi - lo + 1 == c.size:
        return ((1 << c.size) - 1) << lo
    m = 0
    for x in c:
        m |= 1 << int(x)
    return m


def ap(T, d):
    if d[0] == "ind":
        return ap(T, d[1]).indirect(ap(T, d[2]))
    return T[d[0]][(slice(None),) + d[1]]


def build(cores, topo):
    ops, acc, top, cur, nd = [], {}, {"I": 0, "F": 0, "U": 0, "B": 0}, [0], [0] * NR
    CY = PAR["cy"]

    def tiles(buf, *ns):
        out = []
        for n in ns:
            out.append(D(buf, (top[buf], n)))
            top[buf] += (n + 15) // 16 * 16
        assert top[buf] <= SCRATCH[buf][1][1], buf
        return out

    def op(r, eng, cost, reads, writes, emit, lat=0.0, sem=None, soft=(), wr=None):
        o = {"id": len(ops), "r": r, "eng": eng, "cost": cost, "lat": lat, "emit": emit, "sem": sem, "deps": set(), "soft": list(soft),
             "wr": wr, "q": cur[0]}
        todo = []
        for d in reads:
            todo += [(r, d[1], False), (r, d[2], False)] if d[0] == "ind" else [(r, d, False)]
        for d in writes:
            todo += [(r, d[1], True), (r, d[2], False)] if d[0] == "ind" else [(x, d, True) for x in (wr or [r])]
        for x, d, w in todo:
            m, bank = bits(d), SCRATCH[d[0]][0] == "psum"
            for (m2, o2, w2) in acc.get((x, d[0]), []):
                if (m & m2 and (w or w2)) or (bank and ops[o2]["eng"] != eng):
                    o["deps"].add(o2)
        for x, d, w in todo:
            m, bank = bits(d), SCRATCH[d[0]][0] == "psum"
            lst = acc.setdefault((x, d[0]), [])
            if bank and w:
                lst[:] = [e for e in lst if e[1] == o["id"] or ops[e[1]]["eng"] == eng]
            if w:
                lst[:] = [e for e in lst if e[0] & ~m]
            lst.append((m, o["id"], w))
        ops.append(o)
        return o["id"]

    def nel(d):
        return cols(d).size

    def vcost(out, a, k):
        if out[0] == "ind":
            return 60 + nel(a) * 4 * CY
        if a[0] == "ind":
            return 60 + nel(out) * 1.7 * CY
        return max(64, nel(out) * k) * CY

    def aps(x):
        return [x] if isinstance(x, tuple) else []

    def val(T, x):
        return ap(T, x) if isinstance(x, tuple) else x

    def tt(r, out, a, b, o):
        k = 1 if (a[0] != "ind" and SCRATCH[a[0]][0] == "psum") else 2
        return op(r, "v", vcost(out, a, k), [a, b], [out], lambda g, T: g.vector.tensor_tensor(ap(T, out), ap(T, a), ap(T, b), o))

    def ts(r, out, a, s1, o0, s2=None, o1=None):
        if o1 is None:
            f = lambda g, T: g.vector.tensor_scalar(ap(T, out), ap(T, a), val(T, s1), None, o0)
        else:
            f = lambda g, T: g.vector.tensor_scalar(ap(T, out), ap(T, a), val(T, s1), val(T, s2), o0, o1)
        return op(r, "v", vcost(out, a, 1), [a] + aps(s1) + aps(s2), [out], f)

    def cp(r, out, a):
        return op(r, "v", vcost(out, a, 1), [a], [out], lambda g, T: g.vector.tensor_copy(ap(T, out), ap(T, a)))

    def ms(r, out, c, k=1.0):
        return op(r, "v", max(64, nel(out) * k) * CY, [], [out], lambda g, T: g.vector.memset(ap(T, out), c))

    def act(r, out, a, fn=ACT.Identity):
        return op(r, "a", 70 + nel(out) * (1.7 if a[0] == "ind" else 1) * CY, [a], [out], lambda g, T: g.scalar.activation(ap(T, out), ap(T, a), fn))

    def iota(r, out, pat, base=0, cm=0):
        return op(r, "g", 130 + 2 * nel(out) * CY, [], [out], lambda g, T: g.iota(ap(T, out), pat, base, cm))

    def asel(r, out, a, pat, cmp, base, cm):
        return op(r, "g", 170 + 2 * nel(out) * CY, [a], [out], lambda g, T: g.affine_select(ap(T, out), ap(T, a), pat, cmp, 0.0, base, cm))

    def dma(r, q, reads, writes, fo, fi, lat, soft=()):
        s = "d%d" % nd[r]
        nd[r] += 1
        f = lambda g, T: (g.sync if q == "s" else g.scalar).dma_start(fo(T), fi(T))
        return op(r, q, 100, reads, writes, f, lat=lat, sem=(s, 16), soft=soft)

    def group(r, out, pairs, k, reads):
        def f(g, T):
            for t, (a, b) in enumerate(pairs):
                last = g.tensor.matmul(ap(T, out), ap(T, a), ap(T, b), t == 0, t == len(pairs) - 1)
            return last
        return op(r, "p", max(64, nel(out)) * k * len(pairs) * CY, reads, [out], f)

    def lookup(r, off, n, gat, bank, out):
        dst, ps, k = sub(GB, gat, 16 * n), D(bank, (0, 4 * n)), sub(K0, 0, 4 * n)
        act(r, dst, ("ind", FT, off))
        group(r, ps, [(BA, sub(BB, 0, 4 * n))] + [(sub(SEL, 128 * t, 128), sub(dst, t, 4 * n, 4)) for t in range(4)], 1, [dst, BA, BB, SEL])
        op(r, "v", max(64, 4 * n) * CY, [k, ps], [out], lambda g, T: g.vector.tensor_tensor_scan(ap(T, out), ap(T, k), ap(T, ps), 0.0, A.mult, A.max))

    def nengines(m):
        return bin(m).count("1")

    def send_all(r, d, sem):
        others = [(r + j) % NR for j in range(1, NR)]
        m = topo.mask(cores[r], cores[others[0]])
        for x in others[1:]:
            m &= topo.mask(cores[r], cores[x])
        ids = [topo.addr(cores[x])[:2] for x in others]

        def f(g, T):
            tr = RemoteDMATransfer(dst_ids=[DstId(rid=a, pnc=b) for a, b in ids], dma_engine_mask=m, remote_sem=T.sem[sem],
                                   srcs=[ap(T, d)], dsts=[ap(T, d) for _ in ids])
            return g.remote_dma_fused([tr], local_sem=T.sem["sent"])
        o = op(r, "g", PAR["issue"], [d], [d], f, lat=PAR["all"], sem=(sem, nengines(m)), wr=others)
        ops[o]["sent"] = nengines(m)

    def send_one(r, x, src, dst, sem):
        m = topo.mask(cores[r], cores[x])
        total = sum(nengines(topo.mask(cores[z], cores[x])) for z in range(NR) if z != x)
        a, b = topo.addr(cores[x])[:2]
        f = lambda g, T: g.remote_dma(ap(T, dst), ap(T, src), T.sem[sem], T.sem["sent"], b, a, m)
        o = op(r, "g", PAR["issue"], [src], [dst], f, lat=PAR["one"], sem=(sem, total), wr=[x])
        ops[o]["sent"] = nengines(m)

    ONE, K0, GS, ZF, GN, PIF, PXF, P16, LIM1, LIM2, PY = tiles("F", 128, 128, 8, 240, 8, 1, 1, 1, 6, 6, 2)
    PC, INC0, C1, SLC, FS0, FS, TT, UU, G, YL, YS = tiles("F", 48, 64, 48, 48, 64, 192, 48, 48, 64, 96, 192)
    MU, DL, XM, TI, EE, QB, RR, T16, ZZ, MR, XR = tiles("F", 48, 64, 64, 64, 48, 48, 48, 48, 64, 336, 336)
    LT, LP, LG, GSB, ONEB, NEGB, EQ0, EQ, BA, BB, SEL, ZB, MX, GB, M = tiles("B", 256, 48, 768, 8, 128, 128, 128, 128, 128, 128, 512, 240, 512, 768, 64)
    PI0, PI1, PX, LIMI, STI, RAW, RAW2, I16, PC0, SL0 = tiles("I", 1, 1, 4, 6, 64, 48, 48, 16, 48, 48)
    LV5, LV7, XF, GM, DD, TP, DQ, E6 = tiles("I", 160, 336, 96, 48, 48, 16, 96, 16)
    LI, LST, STU = tiles("U", 48, 48, 64)
    LM, LR, LE, LX = sub(LST, 0, 4), sub(LST, 4, 10), sub(LST, 14, 21), sub(LST, 36, 4)
    POS, INC = sub(PC, 0, 16), sub(INC0, 0, 32)
    LA = {(c, q): tiles("U", 64)[0] for c in range(1, NCY + 2) for q in range(NR)}
    LK = tiles("F", 112, 112, 112, 112)
    RL = {c: tiles("F", 144)[0] for c in range(1, NCY + 1)}
    PS = {(c, j): tiles("F", 48)[0] for c in range(1, NCY + 1) for j in range(1, NR)}
    R = {c: tiles("F", 48)[0] for c in range(1, NCY + 2)}
    FR, FT, PM, AST = D("fr", (0, W)), D("ft", (0, W)), D("pm", (0, 64)), D("pt", (0, 112))

    for r in range(NR):
        cur[0] = 0
        fi, fh, fl = D("fi", (0, 512)), D("fh", (0, 512)), D("fl", (0, 512))
        d0 = dma(r, "s", [], [fi], lambda T: T["fi"][:, :], lambda T: T.first[:, :], 2600)
        dma(r, "a", [], [STI], lambda T: ap(T, STI), lambda T: T.start[:, :], 2300)
        dma(r, "a", [], [LIMI], lambda T: ap(T, LIMI), lambda T: T.lim[:, :], 2300)
        d1 = dma(r, "s", [], [sub(FR, 0, W // 2)], lambda T: T["fr"][:, 0:W // 2], lambda T: T.frag[:, 0:W // 2], 6000, soft=[d0])
        ms(r, sub(FT, 0, 1024), 0.0, 0.5)
        act(r, sub(FT, 6144, 1024), sub(FT, 0, 1024))
        act(r, sub(FT, 7168, 1024), sub(FT, 0, 1024))
        ms(r, sub(FT, 1024, 5120), 0.0, 0.5)
        cp(r, fh, fi)
        tt(r, fl, fi, fh, A.subtract)
        d2 = dma(r, "s", [fh, FT], [], lambda T: T["ft"][0:128:16, :], lambda T: T["fh"][:, :], 2600, soft=[d1])
        d3 = dma(r, "s", [fl, FT], [], lambda T: T["ft"][1:128:16, :], lambda T: T["fl"][:, :], 2600, soft=[d2])
        acc[(r, "ft")] = [(bits(FT), d2, True), (bits(FT), d3, True)]
        dma(r, "s", [], [sub(FR, W // 2, W // 2)], lambda T: T["fr"][:, W // 2:W], lambda T: T.frag[:, W // 2:W], 6000, soft=[d3])
        ms(r, ONEB, 1.0)
        ms(r, NEGB, -BIG)
        ms(r, ONE, 1.0)
        asel(r, EQ0, ONEB, [[-16, 8], [0, 16]], A.is_ge, 0, 1)
        asel(r, EQ, EQ0, [[16, 8], [0, 16]], A.is_ge, 15, -1)
        for t in range(4):
            asel(r, sub(SEL, 128 * t, 128), EQ, [[0, 32], [1, 4]], A.is_equal, -t, 0)
        asel(r, BA, ONEB, [[0, 8], [1, 4], [0, 4]], A.is_equal, 0, -1)
        asel(r, BB, NEGB, [[0, 32], [1, 4]], A.not_equal, 0, -1)
        asel(r, K0, ONE, [[0, 32], [1, 4]], A.is_gt, 0, 0)
        act(r, GS, sub(EQ, 0, 8, 16))
        act(r, GSB, sub(EQ, 0, 8, 16))
        ts(r, GN, GS, -1.0, A.mult)
        iota(r, PI0, [[0, 1]], 0, 1)
        ts(r, PI1, PI0, 15, A.bitwise_and)
        cp(r, PIF, PI1)
        ts(r, sub(PX, 0, 1), PI0, 7, A.bitwise_and)
        ts(r, sub(PX, 1, 1), PI0, 8, A.bitwise_and)
        ts(r, sub(PX, 2, 1), PI0, 4, A.arith_shift_right)
        cp(r, PY, sub(PX, 1, 2))
        ts(r, PXF, sub(PX, 0, 1), 64.0, A.mult, sub(PY, 0, 1), A.add)
        ts(r, PXF, PXF, sub(PY, 1, 1), A.add)
        iota(r, sub(RAW, 0, 9), [[0, 9]])
        iota(r, sub(RAW, 9, 5), [[0, 5]], 32)
        iota(r, sub(RAW, 14, 21), [[32, 3], [0, 7]])
        iota(r, sub(RAW, 35, 5), [[16, 5]], -16)
        ts(r, sub(RAW2, 0, 36), sub(RAW, 0, 36), PIF, A.add)
        ts(r, sub(RAW2, 36, 4), sub(RAW, 36, 4), PXF, A.add)
        cp(r, sub(LST, 0, 40), sub(RAW2, 0, 40))
        iota(r, I16, [[1, 16]])
        ms(r, ZF, 0.0)
        ts(r, sub(ZF, 112, 16), I16, PIF, A.is_equal)
        act(r, ZB, ZF)
        ms(r, MX, 0.0, 0.5)
        iota(r, PC0, [[256, 3], [16, 16]])
        ts(r, PC, PC0, PIF, A.add)
        iota(r, SL0, [[1, 3], [0, 16]])
        iota(r, LV5, [[0, 2], [1, 5], [0, 16]])
        iota(r, LV7, [[0, 3], [1, 7], [0, 16]])
        ts(r, SLC, SL0, 32768.0, A.mult)
        ms(r, sub(INC0, 0, 16), float(STEP))
        ms(r, sub(INC0, 16, 16), 1.0)
        ms(r, sub(INC0, 32, 32), 0.0)
        ms(r, sub(C1, 0, 16), float(STEP))
        ms(r, sub(C1, 16, 32), 0.0)
        ms(r, AST, 10.0)
        ts(r, P16, PIF, 16.0, A.mult)
        ms(r, LT, 0.0, 0.5)
        ms(r, LP, 0.0, 0.5)
        ts(r, LIM1, LIMI, float(7 * 2 ** 21), A.min, 1.0, A.add)
        cp(r, sub(LP, 0, 6), LIM1)
        tt(r, LIM2, LIM1, sub(LP, 0, 6), A.subtract)
        cp(r, sub(LP, 16, 6), LIM2)
        tt(r, sub(LP, 32, 6), LIM2, sub(LP, 16, 6), A.subtract)
        a0, b0 = LT[1][0].start, LP[1][0].start
        dl = [dma(r, "a", [LP, LT], [], lambda T, j=j: T["B"][j:128:16, a0:a0 + 256], lambda T, j=j: T["B"][:, b0 + 16 * j:b0 + 16 * j + 16], 2400) for j in range(3)]
        acc[(r, "B")] += [(bits(LT), d, True) for d in dl]
        cp(r, STU, STI)
        lookup(r, sub(STU, 16 * r, 16), 16, 256, "pb", FS0)
        F0 = sub(FS0, 3, 16, 4)
        cp(r, sub(R[1], 16, 16), F0)
        ts(r, TP, F0, float(STEP), A.add)
        ts(r, TP, TP, W - 1, A.bitwise_and)
        cp(r, sub(R[1], 32, 16), TP)
        cp(r, sub(LA[1, r], 16, 32), sub(R[1], 16, 32))
        ts(r, D("cs1", 1, (32, 16)), F0, float(W), A.add)
        ts(r, D("cs1", 1, (48, 16)), sub(STI, 16 * r, 16), 16.0, A.mult, 11.0, A.add)
        tt(r, D("cs1", 1, (64, 32)), D("cs1", 1, (32, 32)), INC, A.subtract)
        tt(r, D("cs1", 1, (96, 32)), D("cs1", 1, (32, 32)), INC, A.subtract)
    for r in range(NR):
        send_all(r, sub(LA[1, r], 16, 32), "la1_%d" % r)

    def nstep(r, cs, k, drop, row, dst):
        tp, pg = D(cs, row, (32, 64)), D(cs, row, (64, 64))
        if not drop:
            tt(r, dst, tp, INC0, A.add)
            return
        gm, mu = sub(GM, 16 * k, 16), sub(MU, 16 * k, 16)
        ts(r, gm, D(cs, row, (48, 16)), 15, A.bitwise_and)
        ts(r, mu, gm, 15.0, A.is_equal)
        tt(r, DL, pg, tp, A.subtract)
        tt(r, TI, tp, INC0, A.add)
        tt(r, XM, ("ind", mu, LM), DL, A.mult)
        tt(r, dst, TI, XM, A.add)

    for c in range(1, NCY + 1):
        cs, cl, last = "cs%d" % c, "cl%d" % c, c == NCY
        s1 = 3 * c - 2
        for r in range(NR):
            cur[0] = r
            lookup(r, sub(LA[c, r], 16, 16), 16, 0, "pa", sub(FS, 0, 64))
            cp(r, sub(LA[c, r], 48, 16), sub(FS, 3, 16, 4))
            send_all(r, sub(LA[c, r], 48, 16), "lb%d_%d" % (c, r))
            if not last:
                lookup(r, sub(LA[c, r], 32, 32), 32, 256, "pb", sub(FS, 64, 128))
        for q in range(NR):
            for r in range(NR):
                cur[0] = q
                L, bank = "L%d" % q, "pe%d" % q
                slot = [D(L, (256 * (s1 + e), 256)) for e in range(3)]
                if c == 1:
                    base = D(L, (0, 256))
                    act(r, base, ("ind", FR, sub(STU, 16 * q, 16)))
                else:
                    base = D("S", (256 * q, 256))
                    act(r, base, ("ind", D(L, (0, 256 * s1)), sub(LA[c, q], 0, 16)))
                tt(r, slot[0], ("ind", FR, sub(LA[c, q], 16, 16)), base, A.add)
                tt(r, slot[1], ("ind", FR, sub(LA[c, q], 32, 16)), base, A.add)
                tt(r, slot[2], ("ind", FR, sub(LA[c, q], 48, 16)), slot[0], A.add)
                for e in range(3):
                    a = D("ab", (768 * q + 256 * e, 256))
                    act(r, a, slot[e], ACT.Abs)
                    for b in range(2 if r != q else 0):
                        group(r, D(bank, (16 * e + 8 * b, 8)), [(sub(a, 128 * b, 128), GS)], 4, [a, GS])
                j = (r - q) % NR
                if j:
                    act(r, PS[c, j], D(bank, (0, 48)))
                    send_one(r, q, PS[c, j], sub(RL[c], 48 * (j - 1), 48), "pr%d" % c)
        for r in range(NR):
            cur[0] = r
            Fv = sub(FS, 3, 48, 4)
            nstep(r, cs, 0, c >= 3, 1, D(cs, 2, (32, 64)))
            if c >= 3:
                cp(r, D(cs, 2, (96, 32)), D(cs, 1, (96, 32)))
            nstep(r, cs, 1, c >= 3, 2, D(cs, 0, (0, 64)))
            cp(r, D(cs, 0, (64, 32)), D(cs, 1, (96, 32)))
            cp(r, D(cs, 3, (64, 32)), D(cs, 1, (32, 32)))
            ts(r, sub(DD, 0, 32), D(cs, (1, 2), (32, 16)), 20, A.arith_shift_right)
            ts(r, sub(DD, 32, 16), sub(DD, 0, 16), 1.0, A.add)
            if c >= 3:
                ts(r, sub(EE, 0, 32), sub(MU, 0, 32), 8.0, A.mult)
                tt(r, sub(EE, 0, 32), sub(EE, 0, 32), sub(DD, 0, 32), A.add)
                ts(r, sub(LI, 0, 32), sub(EE, 0, 32), P16, A.add)
                ts(r, sub(LI, 32, 16), sub(DD, 32, 16), P16, A.add)
            else:
                ts(r, LI, DD, P16, A.add)
            U0 = D("pe%d" % r, (0, 48))
            for e in range(3):
                act(r, sub(LG, 256 * e, 256), ("ind", LT, sub(LI, 16 * e, 16)))
                for b in range(2):
                    a, lg = D("ab", (768 * r + 256 * e + 128 * b, 128)), sub(LG, 256 * e + 128 * b, 128)
                    group(r, sub(U0, 16 * e + 8 * b, 8), [(lg, GSB), (a, GN)], 2.5, [a, lg, GSB, GN])
            ts(r, QB, DD, float(2 ** 20), A.mult, float(2 ** 20 + W + s1 * 2 ** 15), A.add)
            if last:
                tt(r, D(cs, (1, 3), (0, 16)), QB, SLC, A.add)
            else:
                tt(r, QB, QB, SLC, A.add)
                tt(r, D(cs, (1, 3), (0, 16)), QB, Fv, A.add)
            if c >= 3:
                ts(r, sub(T16, 0, 32), sub(R[c], 16, 32), 16.0, A.mult, 11.0, A.add)
                ts(r, sub(T16, 32, 16), sub(FS, 3, 16, 4), 16.0, A.mult, 11.0, A.add)
                ts(r, RR, DD, 5.0, A.is_equal, 5.0, A.mult)
                tt(r, D(cs, (1, 3), (16, 16)), T16, RR, A.add)
            else:
                ts(r, D(cs, (1, 2), (16, 16)), sub(R[c], 16, 32), 16.0, A.mult, 11.0, A.add)
                ts(r, D(cs, 3, (16, 16)), sub(FS, 3, 16, 4), 16.0, A.mult, 11.0, A.add)
            cp(r, D(cs, 3, (32, 32)), D(cs, 1, (0, 32)))
            tt(r, D(cs, 1, (0, 32)), D(cs, 1, (0, 32)), INC, A.add)
            t2q = D(cs, 0, (0, 16))
            t3q = t2q if last else D(cl, 0, (32, 16))
            if not last:
                if c >= 2:
                    gm, mu = sub(GM, 32, 16), sub(MU, 32, 16)
                    ts(r, gm, D(cs, 0, (16, 16)), 15, A.bitwise_and)
                    ts(r, mu, gm, 15.0, A.is_equal)
                    tt(r, sub(DL, 0, 16), D(cs, 0, (32, 16)), t2q, A.subtract)
                    ts(r, sub(TI, 0, 16), t2q, float(STEP), A.add)
                    tt(r, sub(XM, 0, 16), mu, sub(DL, 0, 16), A.mult)
                    tt(r, t3q, sub(TI, 0, 16), sub(XM, 0, 16), A.add)
                else:
                    ts(r, t3q, t2q, float(STEP), A.add)
                cp(r, D(cl, 0, (16, 16)), t2q)
            ts(r, TP, t3q, 7, A.arith_shift_right, 0x1F00, A.bitwise_and)
            tt(r, D(cl, 0, (0, 16)), TP, POS, A.add)
            ts(r, D(cl, (1, 3), (0, 16)), PC, 256.0 * s1, A.add)
            if not last:
                tt(r, D(cl, (1, 3), (16, 16)), Fv, C1, A.add)
                ts(r, D(cl, (1, 3), (32, 16)), D(cl, (1, 3), (16, 16)), float(STEP), A.add)
                ts(r, D(cl, (0, 4), (16, 32)), D(cl, (0, 4), (16, 32)), W - 1, A.bitwise_and)
            tt(r, TT, sub(RL[c], 0, 48), sub(RL[c], 48, 48), A.add)
            tt(r, UU, U0, sub(RL[c], 96, 48), A.subtract)
            tt(r, sub(G, 16, 48), TT, UU, A.is_lt)
            tt(r, sub(G, 0, 16), sub(TT, 0, 16), sub(UU, 0, 16), A.is_ge)
            tt(r, sub(M, 0, 32), sub(G, 0, 32), sub(G, 32, 32), A.is_gt)
            tt(r, sub(M, 32, 32), sub(G, 0, 32), sub(G, 32, 32), A.min)
            cp(r, ("ind", MX, LX), M)
            group(r, PM, [(sub(ZB, 112 - 16 * h, 128), sub(MX, 64 * h, 64)) for h in range(8)], 1, [MX, ZB])
            n = 16 if last else 48
            for f in range(0, n, 16):
                tt(r, D("xl", (0, 4), (f, 16)), PM, D(cl, (0, 4), (f, 16)), A.mult)
            tt(r, sub(YL, 0, 2 * n), D("xl", (0, 2), (0, n)), D("xl", (2, 2), (0, n)), A.add)
            tt(r, sub(R[c + 1], 0, n), sub(YL, 0, n), sub(YL, n, n), A.add)
            cp(r, sub(LA[c + 1, r], 0, n), sub(R[c + 1], 0, n))
            send_all(r, sub(LA[c + 1, r], 0, n), "la%d_%d" % (c + 1, r))
            for f in range(0, 96, 16):
                tt(r, D("xs", (0, 4), (f, 16)), PM, D(cs, (0, 4), (f, 16)), A.mult)
            tt(r, YS, D("xs", (0, 2), (0, 96)), D("xs", (2, 2), (0, 96)), A.add)
            tt(r, XF if last else D("cs%d" % (c + 1), 1, (32, 96)), sub(YS, 0, 96), sub(YS, 96, 96), A.add)
            if c >= 2:
                ts(r, sub(DQ, 0, 64), D(cs, 1, (64, 64)), 20, A.arith_shift_right)
                cp(r, ZZ, D(cs, 1, (64, 64)))
                tt(r, sub(MR, 0, 160), ("ind", sub(DQ, 0, 64), LR), LV5, A.is_equal)
                tt(r, sub(ZZ, 16, 16), sub(PM, 48, 16), sub(ZZ, 16, 16), A.mult)
                tt(r, sub(XR, 0, 160), ("ind", sub(ZZ, 16, 48), LR), sub(MR, 0, 160), A.mult)
                tt(r, sub(AST, 0, 80), sub(AST, 0, 80), sub(XR, 0, 80), A.max)
                tt(r, sub(AST, 0, 80), sub(AST, 0, 80), sub(XR, 80, 80), A.max)

    for r in range(NR):
        cur[0] = r
        ts(r, DQ, XF, 20, A.arith_shift_right)
        tt(r, MR, ("ind", DQ, LE), LV7, A.is_equal)
        tt(r, XR, ("ind", sub(XF, 16, 80), LE), MR, A.mult)
        for k in range(3):
            tt(r, AST, AST, sub(XR, 112 * k, 112), A.max)
        ts(r, sub(LK[r], 0, 96), sub(AST, 0, 96), 11.0, A.subtract)
        cp(r, E6, sub(AST, 96, 16))
        ts(r, E6, E6, 0x3FFF0, A.bitwise_and)
        ts(r, sub(LK[r], 96, 16), E6, 16.0, A.subtract, -1.0, A.max)
        send_all(r, LK[r], "lb%d_%d" % (NCY + 1, r))
    for r in range(NR):
        for q in range(NR):
            cur[0] = q
            yq = D("Y", (256 * q, 256))
            act(r, yq, ("ind", D("L%d" % q, (0, 256 * (3 * NCY + 1))), sub(LA[NCY + 1, q], 0, 16)))
            dma(r, "s", [yq], [], lambda T, q=q: T.y[:, 256 * q:256 * q + 256], lambda T, yq=yq: ap(T, yq), 2500)
            act(r, D("sk", (0, 7), (16 * q, 16)), LK[q])
        dma(r, "a", [D("sk", (0, 7), (0, 64))], [], lambda T: T.stk[:, :], lambda T: T["sk"][:, :, :], 2800)
    return ops


def arrange(ops):
    n = len(ops)
    succ = [set() for _ in range(n)]
    for o in ops:
        for d in list(o["deps"]) + o["soft"]:
            succ[d].add(o["id"])
    succ = [sorted(s) for s in succ]

    def gap(a, b):
        if a["id"] not in b["deps"]:
            return a["cost"]
        return a["cost"] + a["lat"] + (60.0 if (a["eng"] == b["eng"] and a["r"] == b["r"]) else 120.0)
    prio = [0.0] * n
    for o in reversed(ops):
        prio[o["id"]] = max([gap(o, ops[s]) + prio[s] for s in succ[o["id"]]] + [o["cost"] + o["lat"]])
    x = PAR["seed"]
    for o in ops:
        x = (x * 1103515245 + 12345) % 2147483648
        prio[o["id"]] += PAR["noise"] * x / 2147483648.0 - PAR["shift"] * o["q"]
    left = [len(set(o["deps"]) | set(o["soft"])) for o in ops]
    ready_at, start = [0.0] * n, [0.0] * n
    free, ready, order = {}, {}, []
    for o in ops:
        ready.setdefault((o["r"], o["eng"]), [])
        if left[o["id"]] == 0:
            ready[o["r"], o["eng"]].append(o["id"])
    keys = sorted(ready)
    while len(order) < n:
        t, k = min((max(free.get(k, 0.0), min(ready_at[i] for i in ready[k])), k) for k in keys if ready[k])
        i = max((i for i in ready[k] if ready_at[i] <= t + 40.0), key=lambda i: (prio[i], -i))
        ready[k].remove(i)
        start[i] = max(t, ready_at[i])
        free[k] = start[i] + ops[i]["cost"]
        order.append(i)
        for s in succ[i]:
            ready_at[s] = max(ready_at[s], start[i] + gap(ops[i], ops[s]))
            left[s] -= 1
            if left[s] == 0:
                ready[ops[s]["r"], ops[s]["eng"]].append(s)
    return order, start, max(start[i] + ops[i]["cost"] + ops[i]["lat"] for i in range(n))


def programs(ops, order, start):
    count, known, prog = {}, {}, [[] for _ in range(NR)]
    tail = [{} for _ in range(NR)]
    for i in order:
        o = ops[i]
        r = o["r"]
        kn = known.setdefault((r, o["eng"]), {})
        waits = []
        for d in sorted(o["deps"], key=lambda d: -start[d]):
            p = ops[d]
            s, v = p["done"]
            if kn.get(s, 0) < v:
                waits.append((s, v))
                kn[s] = v
                if p["wr"] is None:
                    for s2, v2 in p["kn"].items():
                        kn[s2] = max(kn.get(s2, 0), v2)
        o["kn"] = dict(kn)
        if o["sem"] is None:
            s = "c" + o["eng"]
            count[(r, s)] = count.get((r, s), 0) + 1
            o["done"] = (s, count[(r, s)])
            inc = (s, 1)
            tail[r][s] = count[(r, s)]
        else:
            o["done"] = o["sem"]
            inc = o["sem"] if o["wr"] is None else None
            for x in (o["wr"] or [r]):
                tail[x][o["sem"][0]] = o["sem"][1]
            if o["wr"] is not None:
                tail[r]["sent"] = tail[r].get("sent", 0) + o["sent"]
        prog[r].append((o["eng"], waits, o["emit"], inc))
    for r in range(NR):
        seen = {}
        for k, kn in known.items():
            if k[0] == r:
                for s, v in kn.items():
                    seen[s] = max(seen.get(s, 0), v)
        tail[r] = [(s, v) for s, v in sorted(tail[r].items()) if seen.get(s, 0) < v]
    return prog, tail


def rank_program(g, core, T, topo):
    rank = T.rank_of(core)
    if rank is None:
        return
    if "p" not in _PLAN:
        ops = build(list(T.cores), topo)
        order, start, _ = arrange(ops)
        _PLAN["p"] = programs(ops, order, start)
    prog, tail = _PLAN["p"]
    queue = {"v": g.vector, "a": g.scalar, "p": g.tensor, "g": g, "s": g.sync}
    for eng, waits, emit, inc in prog[rank]:
        for s, v in waits:
            queue[eng].wait_ge(T.sem[s], v)
        ins = emit(g, T)
        if inc is not None:
            ins.then_inc(T.sem[inc[0]], inc[1])
    for s, v in tail[rank]:
        g.sync.wait_ge(T.sem[s], v)
